import numpy as np, ml_dtypes
CORES = [2,42,66,74,82,90,114]
N = 7
import mx_ref
NC = 384
WID = [208,384,130,128,230,356,356]
BF = ml_dtypes.bfloat16
def setup_inputs(rng):
    def f(*shape):
        return mx_ref.flush((rng.standard_normal(shape, dtype=np.float32) * np.exp2(rng.integers(-2, 3, shape[:-1] + (1,)))).astype(BF))
    return {"w": f(N, 128, 512), "x": f(N, 128, 4 * NC)}
def setup_inputs_blocks(rng):
    d = setup_inputs(rng)
    for k in ("w", "x"): d[k] = mx_ref.spread(d[k], rng, 4)
    return d
def setup_inputs_wide(rng):
    d = setup_inputs(rng)
    for k in ("w", "x"): d[k] = mx_ref.flush((d[k].astype(np.float32) * np.exp2(rng.integers(-8, 9, (N, 1, 1))).astype(np.float32)).astype(BF))
    return d
def setup_inputs_zeros(rng):
    d = setup_inputs(rng); v = d["x"].reshape(N, 128, -1, 4).copy()
    v[np.broadcast_to((rng.random((N, 1, v.shape[2], 1)) < 0.33), v.shape)] = 0
    d["x"] = v.reshape(d["x"].shape)
    return d
def reference(w, x):
    OFF = [sum(WID[:j]) for j in range(N + 1)]
    y = np.zeros((N, 128, OFF[N]), np.float32)
    for r in range(N):
        qw = mx_ref.quantize(w[r])
        for j in range(N):
            y[r][:, OFF[j]:OFF[j + 1]] = mx_ref.matmul(qw, mx_ref.quantize(x[j][:, :4 * WID[j]]))
    return {"y": y}

from concourse.bass import DstId, RemoteDMATransfer
from concourse.mybir import dt

N = 7
SLOT = 384
SCRATCH = {
    "xb": ("sbuf", [128, 4 * SLOT], "bfloat16"),
    "wb": ("sbuf", [128, 512], "bfloat16"),
    "qw": ("sbuf", [128, 128], "float8_e4m3fn_x4"),
    "sw": ("sbuf", [128, 128], "uint8"),
    "qx": ("sbuf", [128, N * SLOT], "float8_e4m3fn_x4"),
    "sx": ("sbuf", [128, N * SLOT], "uint8"),
    "ps": ("psum", [128, 512 * N], "float32"),
    "yb": ("sbuf", [128, 1792], "float32"),
}
SEMAPHORES = ["ldx", "ldw", "qx", "qw", "mm", "cp", "st", "snt"] + ["s%d" % j for j in range(N)] + ["c%d" % j for j in range(N)]

TREES = {
    0: "0: 0o 1 4 5 6 | 0o: 2 3",
    1: "1: 1o 2 5 6 0 | 1o: 3 4",
    2: "2: 2o 3 6 0 1 | 2o: 4 5",
    3: "3: 3o 4 0 1 2 | 3o: 5 6",
    4: "4: 4o 5 1 2 3 | 4o: 6 0",
    5: "5: 5o 6 2 3 4 | 5o: 0 1",
    6: "6: 6o 0 3 4 5 | 6o: 1 2",
}
ROWS_AS_COLS = 150
HOP_AS_COLS = 500

_CACHE = {}


def _spec():
    spec = {}
    for j in range(N):
        tree = {}
        for part in TREES[j].split("|"):
            node, kids = part.split(":")
            tree[node.strip()] = kids.split()
        spec[j] = tree
    return spec


def _bits(m):
    return bin(m).count("1")


def _resolve(node, cores, topo):
    if node.isdigit():
        return cores[int(node)]
    home = cores[int(node[:-1])]
    role = node[-1]
    every = range(topo.CHIPS * topo.CORES_PER_CHIP)
    if role in "mn":
        spot = [c for c in every if topo.mates(topo.chip(c), topo.chip(home))]
    else:
        spot = [c for c in every if topo.chip(c) == topo.chip(home)]
    able = [c for c in spot if c not in cores and all(topo.may_write(c, d) for d in cores)]
    same = [c for c in able if topo.die(c) == topo.die(home)]
    other = [c for c in able if topo.die(c) != topo.die(home)]
    return {"s": same[0], "m": same[0], "o": other[0], "n": other[0], "p": other[1]}[role]


def _groups(src, kids, cores, topo):
    far = [k for k in kids if topo.chip(k) != topo.chip(src)]
    near = [k for k in kids if topo.chip(k) == topo.chip(src)]
    off = 0
    for d in cores:
        if topo.chip(d) != topo.chip(src):
            off = topo.mask(src, d)
    out = []
    if near:
        m = topo.mask(src, near[0])
        out.append((near, (m & ~off) if (far and (m & ~off)) else m))
    if far:
        out.append((far, off))
    return out


def _plan(T, topo):
    if "plan" in _CACHE:
        return _CACHE["plan"]
    cores = list(T.cores)
    wid = list(T.tables["WID"])
    spec = _spec()
    tasks = {}
    need = {}
    when = {}
    for j in range(N):
        cost = wid[j] + ROWS_AS_COLS
        todo = [(str(j), 0)]
        while todo:
            node, t0 = todo.pop(0)
            src = _resolve(node, cores, topo)
            kids = spec[j].get(node, [])
            if not kids:
                continue
            kc = [_resolve(k, cores, topo) for k in kids]
            tasks.setdefault(src, []).append((t0, j, kc))
            for grp, m in _groups(src, kc, cores, topo):
                for i, k in enumerate(grp):
                    need[(k, j)] = _bits(m)
                    when[(k, j)] = t0 + HOP_AS_COLS + (i + 1) * cost
                    todo.append((kids[kc.index(k)], when[(k, j)]))
    for c in tasks:
        tasks[c].sort()
    _CACHE["plan"] = (cores, wid, tasks, need, when)
    return _CACHE["plan"]


def _send(g, T, topo, cores, src, j, w, kids, plane):
    a = j * SLOT
    if plane:
        ap, sem = T.sx[:, a:a + w], T.sem["s%d" % j]
    else:
        ap, sem = T.qx[:, a:a + w].bitcast(dt.uint8), T.sem["c%d" % j]
    trs, n = [], 0
    for grp, m in _groups(src, kids, cores, topo):
        ids = [DstId(rid=topo.addr(k)[0], pnc=topo.addr(k)[1]) for k in grp]
        trs.append(RemoteDMATransfer(dst_ids=ids, dma_engine_mask=m, remote_sem=sem, srcs=[ap], dsts=[ap for _ in grp]))
        n += _bits(m)
    g.remote_dma_fused(trs, local_sem=T.sem.snt)
    return n


def rank_program(g, core, T, topo):
    cores, wid, tasks, need, when = _plan(T, topo)
    mine = tasks.get(core, [])
    rank = T.rank_of(core)
    if rank is None and not mine:
        return
    sem = T.sem
    off = [sum(wid[:j]) for j in range(N + 1)]

    if rank is not None:
        w = wid[rank]
        a = rank * SLOT
        g.sync.dma_start(T.xb[:, :4 * w], T.x[:, :4 * w]).then_inc(sem.ldx, 16)
        g.scalar.dma_start(T.wb[:], T.w[:]).then_inc(sem.ldw, 16)
        g.vector.wait_ge(sem.ldx, 16)
        g.vector.quantize_mx(T.qx[:, a:a + w], T.sx[:, a:a + w], T.xb[:, :4 * w]).then_inc(sem.qx, 1)
        g.vector.wait_ge(sem.ldw, 16)
        g.vector.quantize_mx(T.qw[:], T.sw[:], T.wb[:]).then_inc(sem.qw, 1)

    sent = 0
    for _, j, kids in mine:
        own = rank == j
        if own:
            g.wait_ge(sem.qx, 1)
        else:
            g.wait_ge(sem["s%d" % j], need[(core, j)])
        sent += _send(g, T, topo, cores, core, j, wid[j], kids, True)
        if not own:
            g.wait_ge(sem["c%d" % j], need[(core, j)])
        sent += _send(g, T, topo, cores, core, j, wid[j], kids, False)
    if sent:
        g.wait_ge(sem.snt, sent)

    if rank is None:
        return

    order = [rank] + sorted([j for j in range(N) if j != rank], key=lambda j: when[(core, j)])
    for i, j in enumerate(order):
        a = j * SLOT
        if j == rank:
            g.tensor.wait_ge(sem.qx, 1)
            g.tensor.wait_ge(sem.qw, 1)
        else:
            g.tensor.wait_ge(sem["s%d" % j], need[(core, j)])
            g.tensor.wait_ge(sem["c%d" % j], need[(core, j)])
        bank = T.ps[:, 512 * i:512 * i + wid[j]]
        g.tensor.matmul_mx(bank, T.qw[:], T.sw[:], T.qx[:, a:a + wid[j]], T.sx[:, a:a + wid[j]], True, True).then_inc(sem.mm, 1)
        g.vector.wait_ge(sem.mm, i + 1)
        g.vector.tensor_copy(T.yb[:, off[j]:off[j + 1]], bank).then_inc(sem.cp, 1)
        q = g.sync if i % 2 == 0 else g.scalar
        q.wait_ge(sem.cp, i + 1)
        q.dma_start(T.y[:, off[j]:off[j + 1]], T.yb[:, off[j]:off[j + 1]]).then_inc(sem.st, 16)
    g.sync.wait_ge(sem.st, 16 * N)
